import numpy as np, ml_dtypes
CORES = [122,123,126,250,251,254,378,379,382,506,507,510]
N = 12
R, TK = 32, 128
WID = [96,48,128,16,128,96,64,128,64,16,96,16]
def setup_inputs(rng):
    u = (rng.standard_normal((N, 128, R), dtype=np.float32) / 11).astype(ml_dtypes.bfloat16)
    return {"x": rng.standard_normal((N, 128, TK), dtype=np.float32).astype(ml_dtypes.bfloat16), "u": u, "ut": u.transpose(0, 2, 1).copy(), "vt": rng.standard_normal((N, R, 128), dtype=np.float32).astype(ml_dtypes.bfloat16)}
def setup_inputs_big(rng):
    d = setup_inputs(rng)
    for k in ("x", "u", "ut", "vt"): d[k] = (d[k].astype(np.float32) * 1024.0).astype(d[k].dtype)
    return d
def setup_inputs_small(rng):
    d = setup_inputs(rng)
    for k in ("x", "u", "ut", "vt"): d[k] = (d[k].astype(np.float32) * (1 / 1024.0)).astype(d[k].dtype)
    return d
def setup_inputs_apart(rng):
    d = setup_inputs(rng)
    f = (10.0 ** rng.permutation(np.linspace(-1.5, 1.5, N))).astype(np.float32).reshape(N, 1, 1)
    for k in ("x", "u", "ut", "vt"): d[k] = (d[k].astype(np.float32) * f).astype(d[k].dtype)
    return d
def whole(x, u, ut, vt):
    X, U, VT = x.astype(np.float64), u.astype(np.float64), vt.astype(np.float64)
    y = np.stack([sum(VT[j].T @ (U[j].T @ X[r]) for j in range(N)) for r in range(N)])
    return {"y": y.astype(ml_dtypes.bfloat16)}
def reference(x, u, ut, vt):
    o = whole(x, u, ut, vt)["y"].copy()
    for r in range(N):
        o[r][:, WID[r]:] = np.nan
    return {"y": o}

@@ -1,0 +1,105 @@
+from concourse.bass import DstId, RemoteDMATransfer
+
+D = 128
+SCRATCH = {
+    "uts": ("sbuf", [128, D], "bfloat16"),
+    "vts": ("sbuf", [128, D], "bfloat16"),
+    "xs": ("sbuf", [128, D], "bfloat16"),
+    "ys": ("sbuf", [128, D], "bfloat16"),
+    "pa": ("sbuf", [128, 3 * D], "bfloat16"),
+    "pb": ("sbuf", [128, 3 * D], "bfloat16"),
+    "pc": ("sbuf", [128, 3 * D], "bfloat16"),
+    "pp": ("psum", [128, 512], "float32"),
+    "py": ("psum", [128, 512], "float32"),
+}
+SEMAPHORES = ["ld", "xl", "mm", "pc", "sa", "sb", "sd", "sc", "ym", "yc", "st", "loc"]
+
+
+def _bits(m):
+    return bin(m).count("1")
+
+
+def rank_program(g, core, T, topo):
+    rank = T.rank_of(core)
+    if rank is None:
+        return
+    S = T.sem
+    wid = T.tables["WID"][rank]
+    cores = list(T.cores)
+
+    def same_chip(a, b):
+        return topo.host(a) == topo.host(b) and topo.chip(a) == topo.chip(b)
+
+    mine = [c for c in cores if same_chip(c, core)]
+    lane = mine.index(core)
+    sibs = [c for c in mine if c != core]
+    plane = [c for c in cores if topo.same_plane(core, c)]
+    cable = [c for c in cores if not same_chip(c, core) and not topo.same_plane(core, c) and topo.may_write(core, c)]
+    far = cable[lane]
+
+    def dst(c):
+        rid, pid = topo.addr(c, core)
+        return DstId(rid=rid, pnc=pid)
+
+    def slot(buf, k):
+        return buf[:, k * D:(k + 1) * D]
+
+    m_off = topo.mask(core, far)
+    for c in plane:
+        m_off &= topo.mask(core, c)
+    m_on = topo.mask(core, sibs[0]) & topo.mask(core, sibs[1]) & ~m_off
+    n_off, n_on = _bits(m_off), _bits(m_on)
+
+    g.sync.dma_start(T.uts[0:32, :], T.ut[:, :]).then_inc(S.ld, 16)
+    g.scalar.dma_start(T.vts[0:32, :], T.vt[:, :]).then_inc(S.ld, 16)
+    g.scalar.dma_start(T.xs[:, 0:wid], T.x[:, 0:wid]).then_inc(S.xl, 16)
+
+    g.tensor.wait_ge(S.ld, 32)
+    g.tensor.matmul(T.pp[:, 0:D], T.uts[0:32, :], T.vts[0:32, :], start=True, stop=True).then_inc(S.mm, 1)
+    g.vector.wait_ge(S.mm, 1)
+    g.vector.tensor_copy(slot(T.pa, lane), T.pp[:, 0:D]).then_inc(S.pc, 1)
+
+    g.wait_ge(S.pc, 1)
+    g.remote_dma_fused([RemoteDMATransfer(dst_ids=[dst(far)], dma_engine_mask=m_off, remote_sem=S.sb,
+                                          srcs=[slot(T.pa, lane)], dsts=[slot(T.pb, lane)], alu_op=0)],
+                       local_sem=S.loc)
+    g.remote_dma_fused([RemoteDMATransfer(dst_ids=[dst(c) for c in sibs], dma_engine_mask=m_on, remote_sem=S.sa,
+                                          srcs=[slot(T.pa, lane)], dsts=[slot(T.pa, lane) for c in sibs], alu_op=0)],
+                       local_sem=S.loc)
+
+    g.wait_ge(S.sb, n_off)
+    g.remote_dma_fused([
+        RemoteDMATransfer(dst_ids=[dst(c) for c in plane], dma_engine_mask=m_off, remote_sem=S.sc,
+                          srcs=[slot(T.pa, lane), slot(T.pb, lane)], dsts=[slot(T.pc, lane) for c in plane], alu_op=1),
+        RemoteDMATransfer(dst_ids=[dst(c) for c in sibs], dma_engine_mask=m_on, remote_sem=S.sd,
+                          srcs=[slot(T.pb, lane)], dsts=[slot(T.pb, lane) for c in sibs], alu_op=0),
+    ], local_sem=S.loc)
+
+    x = T.xs[:, 0:wid]
+    y = T.py[:, 0:wid]
+    others = [k for k in range(len(mine)) if k != lane]
+    g.tensor.wait_ge(S.xl, 16)
+    g.tensor.wait_ge(S.pc, 1)
+    g.tensor.matmul(y, slot(T.pa, lane), x, start=True, stop=False)
+    g.tensor.wait_ge(S.sa, n_on * len(sibs))
+    for k in others:
+        g.tensor.matmul(y, slot(T.pa, k), x, start=False, stop=False)
+    g.tensor.wait_ge(S.sb, n_off)
+    g.tensor.matmul(y, slot(T.pb, lane), x, start=False, stop=False)
+    g.tensor.wait_ge(S.sd, n_on * len(sibs))
+    for k in others:
+        g.tensor.matmul(y, slot(T.pb, k), x, start=False, stop=False)
+    g.tensor.wait_ge(S.sc, n_off * len(plane))
+    for k in range(len(plane)):
+        last = k == len(plane) - 1
+        mmi = g.tensor.matmul(y, slot(T.pc, k), x, start=False, stop=last)
+        if last:
+            mmi.then_inc(S.ym, 1)
+
+    g.vector.wait_ge(S.ym, 1)
+    g.vector.tensor_copy(T.ys[:, 0:wid], y).then_inc(S.yc, 1)
+    g.sync.wait_ge(S.yc, 1)
+    g.sync.dma_start(T.y[:, 0:wid], T.ys[:, 0:wid]).then_inc(S.st, 16)
+    g.sync.wait_ge(S.st, 16)
+
+    g.wait_ge(S.loc, 2 * n_off + 2 * n_on)

@@ -1,22 +1,39 @@
 from concourse.bass import DstId, RemoteDMATransfer
 
 D = 128
+R = 32
+FW = R * D // 128
+NL = 3
+N_EARLY = (NL - 1) + NL + 1
+N_LATE = NL + (NL - 1)
 SCRATCH = {
-    "uts": ("sbuf", [128, D], "bfloat16"),
-    "vts": ("sbuf", [128, D], "bfloat16"),
+    "fu": ("dram", [128, FW], "bfloat16"),
+    "fv": ("dram", [128, FW], "bfloat16"),
+    "gu": ("dram", [N_EARLY + N_LATE, 128, FW], "bfloat16"),
+    "gv": ("dram", [N_EARLY + N_LATE, 128, FW], "bfloat16"),
+    "uo": ("sbuf", [128, D], "bfloat16"),
+    "vo": ("sbuf", [128, D], "bfloat16"),
+    "ue": ("sbuf", [128, 2 * D], "bfloat16"),
+    "ve": ("sbuf", [128, 2 * D], "bfloat16"),
+    "ul": ("sbuf", [128, 2 * D], "bfloat16"),
+    "vl": ("sbuf", [128, 2 * D], "bfloat16"),
     "xs": ("sbuf", [128, D], "bfloat16"),
+    "ws": ("sbuf", [128, D], "bfloat16"),
     "ys": ("sbuf", [128, D], "bfloat16"),
-    "pa": ("sbuf", [128, 3 * D], "bfloat16"),
-    "pb": ("sbuf", [128, 3 * D], "bfloat16"),
-    "pc": ("sbuf", [128, 3 * D], "bfloat16"),
-    "pp": ("psum", [128, 512], "float32"),
+    "pw": ("psum", [128, 512], "float32"),
     "py": ("psum", [128, 512], "float32"),
 }
-SEMAPHORES = ["ld", "xl", "mm", "pc", "sa", "sb", "sd", "sc", "ym", "yc", "st", "loc"]
+SEMAPHORES = ["fl", "ow", "xl", "el", "ll", "sa", "sw", "sb", "sc", "sd", "mm", "wc", "ym", "yc", "st", "loc"]
 
 
-def _bits(m):
-    return bin(m).count("1")
+def _engines(m):
+    return [1 << b for b in range(m.bit_length()) if (m >> b) & 1]
+
+
+def _halves(m):
+    e = _engines(m)
+    h = len(e) // 2
+    return sum(e[:h]), sum(e[h:]), h
 
 
 def rank_program(g, core, T, topo):
@@ -30,7 +47,24 @@ def rank_program(g, core, T, topo):
     def same_chip(a, b):
         return topo.host(a) == topo.host(b) and topo.chip(a) == topo.chip(b)
 
-    mine = [c for c in cores if same_chip(c, core)]
+    def chip_of(c):
+        return [d for d in cores if same_chip(d, c)]
+
+    def lane_of(c):
+        return chip_of(c).index(c)
+
+    def slot_at(rcv, src):
+        if same_chip(rcv, src):
+            return [c for c in chip_of(rcv) if c != rcv].index(src)
+        if topo.same_plane(rcv, src):
+            return (NL - 1) + lane_of(src)
+        if topo.may_write(src, rcv):
+            if lane_of(src) == lane_of(rcv):
+                return N_EARLY - 1
+            return N_EARLY + NL + [k for k in range(NL) if k != lane_of(rcv)].index(lane_of(src))
+        return N_EARLY + lane_of(src)
+
+    mine = chip_of(core)
     lane = mine.index(core)
     sibs = [c for c in mine if c != core]
     plane = [c for c in cores if topo.same_plane(core, c)]
@@ -41,65 +75,71 @@ def rank_program(g, core, T, topo):
         rid, pid = topo.addr(c, core)
         return DstId(rid=rid, pnc=pid)
 
-    def slot(buf, k):
-        return buf[:, k * D:(k + 1) * D]
-
     m_off = topo.mask(core, far)
     for c in plane:
         m_off &= topo.mask(core, c)
-    m_on = topo.mask(core, sibs[0]) & topo.mask(core, sibs[1]) & ~m_off
-    n_off, n_on = _bits(m_off), _bits(m_on)
+    m_on = ~m_off
+    for c in sibs:
+        m_on &= topo.mask(core, c)
+    off_u, off_v, n_off = _halves(m_off)
+    on_u, on_v, n_on = _halves(m_on)
 
-    g.sync.dma_start(T.uts[0:32, :], T.ut[:, :]).then_inc(S.ld, 16)
-    g.scalar.dma_start(T.vts[0:32, :], T.vt[:, :]).then_inc(S.ld, 16)
+    def send(src_u, src_v, origin, to, m_u, m_v, sem):
+        ids = [dst(c) for c in to]
+        return [
+            RemoteDMATransfer(dst_ids=ids, dma_engine_mask=m_u, remote_sem=sem, srcs=[src_u],
+                              dsts=[T.gu[slot_at(c, origin)] for c in to], alu_op=0),
+            RemoteDMATransfer(dst_ids=ids, dma_engine_mask=m_v, remote_sem=sem, srcs=[src_v],
+                              dsts=[T.gv[slot_at(c, origin)] for c in to], alu_op=0),
+        ]
+
+    g.sync.dma_start(T.fu[:, :], T.ut[:, :]).then_inc(S.fl, 16)
+    g.scalar.dma_start(T.fv[:, :], T.vt[:, :]).then_inc(S.fl, 16)
+    g.sync.dma_start(T.uo[0:R, :], T.ut[:, :]).then_inc(S.ow, 16)
+    g.scalar.dma_start(T.vo[0:R, :], T.vt[:, :]).then_inc(S.ow, 16)
     g.scalar.dma_start(T.xs[:, 0:wid], T.x[:, 0:wid]).then_inc(S.xl, 16)
 
-    g.tensor.wait_ge(S.ld, 32)
-    g.tensor.matmul(T.pp[:, 0:D], T.uts[0:32, :], T.vts[0:32, :], start=True, stop=True).then_inc(S.mm, 1)
+    g.wait_ge(S.fl, 32)
+    g.remote_dma_fused(send(T.fu[:, :], T.fv[:, :], core, [far], off_u, off_v, S.sb), local_sem=S.loc)
+    g.remote_dma_fused(send(T.fu[:, :], T.fv[:, :], core, plane, off_u, off_v, S.sw)
+                       + send(T.fu[:, :], T.fv[:, :], core, sibs, on_u, on_v, S.sa), local_sem=S.loc)
+
+    k_far = slot_at(core, far)
+    g.wait_ge(S.sb, 2 * n_off)
+    g.remote_dma_fused(send(T.gu[k_far], T.gv[k_far], far, plane, off_u, off_v, S.sc)
+                       + send(T.gu[k_far], T.gv[k_far], far, sibs, on_u, on_v, S.sd), local_sem=S.loc)
+
+    pe = N_EARLY * R // 2
+    pl = N_LATE * R // 2
+    for q, gbuf, ebuf, lbuf in ((g.sync, T.gu, T.ue, T.ul), (g.scalar, T.gv, T.ve, T.vl)):
+        q.wait_ge(S.sa, 2 * n_on * len(sibs))
+        q.wait_ge(S.sw, 2 * n_off * len(plane))
+        q.wait_ge(S.sb, 2 * n_off)
+        q.dma_start(ebuf[0:pe, :], gbuf[0:N_EARLY]).then_inc(S.el, 16)
+        q.wait_ge(S.sc, 2 * n_off * len(plane))
+        q.wait_ge(S.sd, 2 * n_on * len(sibs))
+        q.dma_start(lbuf[0:pl, :], gbuf[N_EARLY:N_EARLY + N_LATE]).then_inc(S.ll, 16)
+
+    w = T.pw[:, 0:D]
+    g.tensor.wait_ge(S.ow, 32)
+    g.tensor.matmul(w, T.uo[0:R, :], T.vo[0:R, :], start=True, stop=False)
+    g.tensor.wait_ge(S.el, 32)
+    for c in range(2):
+        g.tensor.matmul(w, T.ue[0:pe, c * D:(c + 1) * D], T.ve[0:pe, c * D:(c + 1) * D], start=False, stop=False)
+    g.tensor.wait_ge(S.ll, 32)
+    g.tensor.matmul(w, T.ul[0:pl, 0:D], T.vl[0:pl, 0:D], start=False, stop=False)
+    g.tensor.matmul(w, T.ul[0:pl, D:2 * D], T.vl[0:pl, D:2 * D], start=False, stop=True).then_inc(S.mm, 1)
     g.vector.wait_ge(S.mm, 1)
-    g.vector.tensor_copy(slot(T.pa, lane), T.pp[:, 0:D]).then_inc(S.pc, 1)
+    g.vector.tensor_copy(T.ws[:, :], w).then_inc(S.wc, 1)
 
-    g.wait_ge(S.pc, 1)
-    g.remote_dma_fused([RemoteDMATransfer(dst_ids=[dst(far)], dma_engine_mask=m_off, remote_sem=S.sb,
-                                          srcs=[slot(T.pa, lane)], dsts=[slot(T.pb, lane)], alu_op=0)],
-                       local_sem=S.loc)
-    g.remote_dma_fused([RemoteDMATransfer(dst_ids=[dst(c) for c in sibs], dma_engine_mask=m_on, remote_sem=S.sa,
-                                          srcs=[slot(T.pa, lane)], dsts=[slot(T.pa, lane) for c in sibs], alu_op=0)],
-                       local_sem=S.loc)
-
-    g.wait_ge(S.sb, n_off)
-    g.remote_dma_fused([
-        RemoteDMATransfer(dst_ids=[dst(c) for c in plane], dma_engine_mask=m_off, remote_sem=S.sc,
-                          srcs=[slot(T.pa, lane), slot(T.pb, lane)], dsts=[slot(T.pc, lane) for c in plane], alu_op=1),
-        RemoteDMATransfer(dst_ids=[dst(c) for c in sibs], dma_engine_mask=m_on, remote_sem=S.sd,
-                          srcs=[slot(T.pb, lane)], dsts=[slot(T.pb, lane) for c in sibs], alu_op=0),
-    ], local_sem=S.loc)
-
-    x = T.xs[:, 0:wid]
     y = T.py[:, 0:wid]
-    others = [k for k in range(len(mine)) if k != lane]
     g.tensor.wait_ge(S.xl, 16)
-    g.tensor.wait_ge(S.pc, 1)
-    g.tensor.matmul(y, slot(T.pa, lane), x, start=True, stop=False)
-    g.tensor.wait_ge(S.sa, n_on * len(sibs))
-    for k in others:
-        g.tensor.matmul(y, slot(T.pa, k), x, start=False, stop=False)
-    g.tensor.wait_ge(S.sb, n_off)
-    g.tensor.matmul(y, slot(T.pb, lane), x, start=False, stop=False)
-    g.tensor.wait_ge(S.sd, n_on * len(sibs))
-    for k in others:
-        g.tensor.matmul(y, slot(T.pb, k), x, start=False, stop=False)
-    g.tensor.wait_ge(S.sc, n_off * len(plane))
-    for k in range(len(plane)):
-        last = k == len(plane) - 1
-        mmi = g.tensor.matmul(y, slot(T.pc, k), x, start=False, stop=last)
-        if last:
-            mmi.then_inc(S.ym, 1)
-
+    g.tensor.wait_ge(S.wc, 1)
+    g.tensor.matmul(y, T.ws[:, :], T.xs[:, 0:wid], start=True, stop=True).then_inc(S.ym, 1)
     g.vector.wait_ge(S.ym, 1)
     g.vector.tensor_copy(T.ys[:, 0:wid], y).then_inc(S.yc, 1)
     g.sync.wait_ge(S.yc, 1)
     g.sync.dma_start(T.y[:, 0:wid], T.ys[:, 0:wid]).then_inc(S.st, 16)
     g.sync.wait_ge(S.st, 16)
 
-    g.wait_ge(S.loc, 2 * n_off + 2 * n_on)
+    g.wait_ge(S.loc, 2 * n_off + 2 * (2 * n_off + 2 * n_on))

@@ -4,26 +4,33 @@ D = 128
 R = 32
 FW = R * D // 128
 NL = 3
-N_EARLY = (NL - 1) + NL + 1
-N_LATE = NL + (NL - 1)
+S_SIB = 0
+S_PL = NL - 1
+S_FAR = NL
+S_MID = NL + 1
+S_LATE = S_MID + 2 * (NL - 1)
+N_SLOT = S_LATE + NL
 SCRATCH = {
     "fu": ("dram", [128, FW], "bfloat16"),
     "fv": ("dram", [128, FW], "bfloat16"),
-    "gu": ("dram", [N_EARLY + N_LATE, 128, FW], "bfloat16"),
-    "gv": ("dram", [N_EARLY + N_LATE, 128, FW], "bfloat16"),
+    "gu": ("dram", [N_SLOT, 128, FW], "bfloat16"),
+    "gv": ("dram", [N_SLOT, 128, FW], "bfloat16"),
     "uo": ("sbuf", [128, D], "bfloat16"),
     "vo": ("sbuf", [128, D], "bfloat16"),
     "ue": ("sbuf", [128, 2 * D], "bfloat16"),
     "ve": ("sbuf", [128, 2 * D], "bfloat16"),
-    "ul": ("sbuf", [128, 2 * D], "bfloat16"),
-    "vl": ("sbuf", [128, 2 * D], "bfloat16"),
+    "um": ("sbuf", [128, D], "bfloat16"),
+    "vm": ("sbuf", [128, D], "bfloat16"),
+    "ul": ("sbuf", [128, D], "bfloat16"),
+    "vl": ("sbuf", [128, D], "bfloat16"),
     "xs": ("sbuf", [128, D], "bfloat16"),
     "ws": ("sbuf", [128, D], "bfloat16"),
     "ys": ("sbuf", [128, D], "bfloat16"),
     "pw": ("psum", [128, 512], "float32"),
     "py": ("psum", [128, 512], "float32"),
 }
-SEMAPHORES = ["fl", "ow", "xl", "el", "ll", "sa", "sw", "sb", "sc", "sd", "mm", "wc", "ym", "yc", "st", "loc"]
+SEMAPHORES = ["flu", "flv", "ow", "xl", "el", "ml", "ll", "sau", "sav", "sbu", "sbv", "swu", "swv", "mu", "mv",
+              "lu", "lv", "mm", "wc", "ym", "yc", "st", "loc", "lo2"]
 
 
 def _engines(m):
@@ -53,16 +60,17 @@ def rank_program(g, core, T, topo):
     def lane_of(c):
         return chip_of(c).index(c)
 
+    def other(rcv, src):
+        return [k for k in range(NL) if k != lane_of(rcv)].index(lane_of(src))
+
     def slot_at(rcv, src):
         if same_chip(rcv, src):
-            return [c for c in chip_of(rcv) if c != rcv].index(src)
+            return S_SIB + other(rcv, src)
         if topo.same_plane(rcv, src):
-            return (NL - 1) + lane_of(src)
+            return S_PL if lane_of(src) == lane_of(rcv) else S_MID + (NL - 1) + other(rcv, src)
         if topo.may_write(src, rcv):
-            if lane_of(src) == lane_of(rcv):
-                return N_EARLY - 1
-            return N_EARLY + NL + [k for k in range(NL) if k != lane_of(rcv)].index(lane_of(src))
-        return N_EARLY + lane_of(src)
+            return S_FAR if lane_of(src) == lane_of(rcv) else S_MID + other(rcv, src)
+        return S_LATE + lane_of(src)
 
     mine = chip_of(core)
     lane = mine.index(core)
@@ -70,6 +78,7 @@ def rank_program(g, core, T, topo):
     plane = [c for c in cores if topo.same_plane(core, c)]
     cable = [c for c in cores if not same_chip(c, core) and not topo.same_plane(core, c) and topo.may_write(core, c)]
     far = cable[lane]
+    near = plane[lane]
 
     def dst(c):
         rid, pid = topo.addr(c, core)
@@ -81,44 +90,53 @@ def rank_program(g, core, T, topo):
     m_on = ~m_off
     for c in sibs:
         m_on &= topo.mask(core, c)
-    off_u, off_v, n_off = _halves(m_off)
-    on_u, on_v, n_on = _halves(m_on)
+    off_a, off_b, n_off = _halves(m_off)
+    on_a, on_b, n_on = _halves(m_on)
 
-    def send(src_u, src_v, origin, to, m_u, m_v, sem):
-        ids = [dst(c) for c in to]
-        return [
-            RemoteDMATransfer(dst_ids=ids, dma_engine_mask=m_u, remote_sem=sem, srcs=[src_u],
-                              dsts=[T.gu[slot_at(c, origin)] for c in to], alu_op=0),
-            RemoteDMATransfer(dst_ids=ids, dma_engine_mask=m_v, remote_sem=sem, srcs=[src_v],
-                              dsts=[T.gv[slot_at(c, origin)] for c in to], alu_op=0),
-        ]
+    def send(src, gbuf, origin, to, m, sem):
+        return RemoteDMATransfer(dst_ids=[dst(c) for c in to], dma_engine_mask=m, remote_sem=sem, srcs=[src],
+                                 dsts=[gbuf[slot_at(c, origin)] for c in to], alu_op=0)
 
-    g.sync.dma_start(T.fu[:, :], T.ut[:, :]).then_inc(S.fl, 16)
-    g.scalar.dma_start(T.fv[:, :], T.vt[:, :]).then_inc(S.fl, 16)
+    g.sync.dma_start(T.fu[:, :], T.ut[:, :]).then_inc(S.flu, 16)
+    g.scalar.dma_start(T.fv[:, :], T.vt[:, :]).then_inc(S.flv, 16)
     g.sync.dma_start(T.uo[0:R, :], T.ut[:, :]).then_inc(S.ow, 16)
     g.scalar.dma_start(T.vo[0:R, :], T.vt[:, :]).then_inc(S.ow, 16)
     g.scalar.dma_start(T.xs[:, 0:wid], T.x[:, 0:wid]).then_inc(S.xl, 16)
 
-    g.wait_ge(S.fl, 32)
-    g.remote_dma_fused(send(T.fu[:, :], T.fv[:, :], core, [far], off_u, off_v, S.sb), local_sem=S.loc)
-    g.remote_dma_fused(send(T.fu[:, :], T.fv[:, :], core, plane, off_u, off_v, S.sw)
-                       + send(T.fu[:, :], T.fv[:, :], core, sibs, on_u, on_v, S.sa), local_sem=S.loc)
+    g.wait_ge(S.flu, 16)
+    g.remote_dma_fused([send(T.fu[:, :], T.gu, core, [far], off_a, S.sbu),
+                        send(T.fu[:, :], T.gu, core, [near], off_b, S.swu)], local_sem=S.loc)
+    g.wait_ge(S.flv, 16)
+    g.remote_dma_fused([send(T.fv[:, :], T.gv, core, [far], off_a, S.sbv),
+                        send(T.fv[:, :], T.gv, core, [near], off_b, S.swv)], local_sem=S.loc)
+    g.remote_dma_fused([send(T.fu[:, :], T.gu, core, sibs, on_a, S.sau),
+                        send(T.fv[:, :], T.gv, core, sibs, on_b, S.sav)], local_sem=S.loc)
 
-    k_far = slot_at(core, far)
-    g.wait_ge(S.sb, 2 * n_off)
-    g.remote_dma_fused(send(T.gu[k_far], T.gv[k_far], far, plane, off_u, off_v, S.sc)
-                       + send(T.gu[k_far], T.gv[k_far], far, sibs, on_u, on_v, S.sd), local_sem=S.loc)
+    g.wait_ge(S.sbu, n_off)
+    g.wait_ge(S.swu, n_off)
+    g.remote_dma_fused([send(T.gu[S_FAR], T.gu, far, plane, off_b, S.lu),
+                        send(T.gu[S_FAR], T.gu, far, sibs, on_a, S.mu),
+                        send(T.gu[S_PL], T.gu, near, sibs, on_b, S.mu)], local_sem=S.loc)
+    g.wait_ge(S.sbv, n_off)
+    g.wait_ge(S.swv, n_off)
+    g.remote_dma_fused([send(T.gv[S_FAR], T.gv, far, plane, off_a | off_b, S.lv),
+                        send(T.gv[S_FAR], T.gv, far, sibs, on_a, S.mv),
+                        send(T.gv[S_PL], T.gv, near, sibs, on_b, S.mv)], local_sem=S.lo2)
+    n_lo2 = 2 * n_off + 2 * n_on
 
-    pe = N_EARLY * R // 2
-    pl = N_LATE * R // 2
-    for q, gbuf, ebuf, lbuf in ((g.sync, T.gu, T.ue, T.ul), (g.scalar, T.gv, T.ve, T.vl)):
-        q.wait_ge(S.sa, 2 * n_on * len(sibs))
-        q.wait_ge(S.sw, 2 * n_off * len(plane))
-        q.wait_ge(S.sb, 2 * n_off)
-        q.dma_start(ebuf[0:pe, :], gbuf[0:N_EARLY]).then_inc(S.el, 16)
-        q.wait_ge(S.sc, 2 * n_off * len(plane))
-        q.wait_ge(S.sd, 2 * n_on * len(sibs))
-        q.dma_start(lbuf[0:pl, :], gbuf[N_EARLY:N_EARLY + N_LATE]).then_inc(S.ll, 16)
+    pe = (S_MID - S_SIB) * R // 2
+    pm = (S_LATE - S_MID) * R
+    pl = (N_SLOT - S_LATE) * R
+    for q, gbuf, ebuf, mbuf, lbuf, sa, sm, sl, nl in (
+            (g.sync, T.gu, T.ue, T.um, T.ul, S.sau, S.mu, S.lu, n_off),
+            (g.scalar, T.gv, T.ve, T.vm, T.vl, S.sav, S.mv, S.lv, 2 * n_off)):
+        q.wait_ge(sa, n_on * len(sibs))
+        q.wait_ge(S.lo2, n_lo2)
+        q.dma_start(ebuf[0:pe, :], gbuf[S_SIB:S_MID]).then_inc(S.el, 16)
+        q.wait_ge(sm, 2 * n_on * len(sibs))
+        q.dma_start(mbuf[0:pm, :], gbuf[S_MID:S_LATE]).then_inc(S.ml, 16)
+        q.wait_ge(sl, nl * len(plane))
+        q.dma_start(lbuf[0:pl, :], gbuf[S_LATE:N_SLOT]).then_inc(S.ll, 16)
 
     w = T.pw[:, 0:D]
     g.tensor.wait_ge(S.ow, 32)
@@ -126,9 +144,10 @@ def rank_program(g, core, T, topo):
     g.tensor.wait_ge(S.el, 32)
     for c in range(2):
         g.tensor.matmul(w, T.ue[0:pe, c * D:(c + 1) * D], T.ve[0:pe, c * D:(c + 1) * D], start=False, stop=False)
+    g.tensor.wait_ge(S.ml, 32)
+    g.tensor.matmul(w, T.um[0:pm, :], T.vm[0:pm, :], start=False, stop=False)
     g.tensor.wait_ge(S.ll, 32)
-    g.tensor.matmul(w, T.ul[0:pl, 0:D], T.vl[0:pl, 0:D], start=False, stop=False)
-    g.tensor.matmul(w, T.ul[0:pl, D:2 * D], T.vl[0:pl, D:2 * D], start=False, stop=True).then_inc(S.mm, 1)
+    g.tensor.matmul(w, T.ul[0:pl, :], T.vl[0:pl, :], start=False, stop=True).then_inc(S.mm, 1)
     g.vector.wait_ge(S.mm, 1)
     g.vector.tensor_copy(T.ws[:, :], w).then_inc(S.wc, 1)
 
@@ -142,4 +161,5 @@ def rank_program(g, core, T, topo):
     g.sync.dma_start(T.y[:, 0:wid], T.ys[:, 0:wid]).then_inc(S.st, 16)
     g.sync.wait_ge(S.st, 16)
 
-    g.wait_ge(S.loc, 2 * n_off + 2 * (2 * n_off + 2 * n_on))
+    g.wait_ge(S.loc, 2 * (2 * n_off) + 2 * n_on + (n_off + 2 * n_on))
+    g.wait_ge(S.lo2, n_lo2)

from concourse.bass import DstId, RemoteDMATransfer

D = 128
R = 32
FW = R * D // 128
NL = 3
S_SIB = 0
S_PL = NL - 1
S_FAR = NL
S_MID = NL + 1
S_LATE = S_MID + 2 * (NL - 1)
N_SLOT = S_LATE + NL
SCRATCH = {
    "fu": ("dram", [128, FW], "bfloat16"),
    "fv": ("dram", [128, FW], "bfloat16"),
    "gu": ("dram", [N_SLOT, 128, FW], "bfloat16"),
    "gv": ("dram", [N_SLOT, 128, FW], "bfloat16"),
    "uo": ("sbuf", [128, D], "bfloat16"),
    "vo": ("sbuf", [128, D], "bfloat16"),
    "ue": ("sbuf", [128, 2 * D], "bfloat16"),
    "ve": ("sbuf", [128, 2 * D], "bfloat16"),
    "um": ("sbuf", [128, D], "bfloat16"),
    "vm": ("sbuf", [128, D], "bfloat16"),
    "ul": ("sbuf", [128, D], "bfloat16"),
    "vl": ("sbuf", [128, D], "bfloat16"),
    "xs": ("sbuf", [128, D], "bfloat16"),
    "ws": ("sbuf", [128, D], "bfloat16"),
    "ys": ("sbuf", [128, D], "bfloat16"),
    "pw": ("psum", [128, 512], "float32"),
    "py": ("psum", [128, 512], "float32"),
}
SEMAPHORES = ["flu", "flv", "ow", "xl", "el", "ml", "ll", "sau", "sav", "sbu", "sbv", "swu", "swv", "mu", "mv",
              "lu", "lv", "mm", "wc", "ym", "yc", "st", "loc", "lo2"]


def _engines(m):
    return [1 << b for b in range(m.bit_length()) if (m >> b) & 1]


def _halves(m):
    e = _engines(m)
    h = len(e) // 2
    return sum(e[:h]), sum(e[h:]), h


def rank_program(g, core, T, topo):
    rank = T.rank_of(core)
    if rank is None:
        return
    S = T.sem
    wid = T.tables["WID"][rank]
    cores = list(T.cores)

    def same_chip(a, b):
        return topo.host(a) == topo.host(b) and topo.chip(a) == topo.chip(b)

    def chip_of(c):
        return [d for d in cores if same_chip(d, c)]

    def lane_of(c):
        return chip_of(c).index(c)

    def other(rcv, src):
        return [k for k in range(NL) if k != lane_of(rcv)].index(lane_of(src))

    def slot_at(rcv, src):
        if same_chip(rcv, src):
            return S_SIB + other(rcv, src)
        if topo.same_plane(rcv, src):
            return S_PL if lane_of(src) == lane_of(rcv) else S_MID + (NL - 1) + other(rcv, src)
        if topo.may_write(src, rcv):
            return S_FAR if lane_of(src) == lane_of(rcv) else S_MID + other(rcv, src)
        return S_LATE + lane_of(src)

    mine = chip_of(core)
    lane = mine.index(core)
    sibs = [c for c in mine if c != core]
    plane = [c for c in cores if topo.same_plane(core, c)]
    cable = [c for c in cores if not same_chip(c, core) and not topo.same_plane(core, c) and topo.may_write(core, c)]
    far = cable[lane]
    near = plane[lane]

    def dst(c):
        rid, pid = topo.addr(c, core)
        return DstId(rid=rid, pnc=pid)

    m_off = topo.mask(core, far)
    for c in plane:
        m_off &= topo.mask(core, c)
    m_on = ~m_off
    for c in sibs:
        m_on &= topo.mask(core, c)
    off_a, off_b, n_off = _halves(m_off)
    on_a, on_b, n_on = _halves(m_on)

    def send(src, gbuf, origin, to, m, sem):
        return RemoteDMATransfer(dst_ids=[dst(c) for c in to], dma_engine_mask=m, remote_sem=sem, srcs=[src],
                                 dsts=[gbuf[slot_at(c, origin)] for c in to], alu_op=0)

    g.sync.dma_start(T.fu[:, :], T.ut[:, :]).then_inc(S.flu, 16)
    g.scalar.dma_start(T.fv[:, :], T.vt[:, :]).then_inc(S.flv, 16)
    g.sync.dma_start(T.uo[0:R, :], T.ut[:, :]).then_inc(S.ow, 16)
    g.scalar.dma_start(T.vo[0:R, :], T.vt[:, :]).then_inc(S.ow, 16)
    g.scalar.dma_start(T.xs[:, 0:wid], T.x[:, 0:wid]).then_inc(S.xl, 16)

    g.wait_ge(S.flu, 16)
    g.remote_dma_fused([send(T.fu[:, :], T.gu, core, [far], off_a, S.sbu),
                        send(T.fu[:, :], T.gu, core, [near], off_b, S.swu)], local_sem=S.loc)
    g.wait_ge(S.flv, 16)
    g.remote_dma_fused([send(T.fv[:, :], T.gv, core, [far], off_a, S.sbv),
                        send(T.fv[:, :], T.gv, core, [near], off_b, S.swv)], local_sem=S.loc)
    g.remote_dma_fused([send(T.fu[:, :], T.gu, core, sibs, on_a, S.sau),
                        send(T.fv[:, :], T.gv, core, sibs, on_b, S.sav)], local_sem=S.loc)

    g.wait_ge(S.sbu, n_off)
    g.wait_ge(S.swu, n_off)
    g.remote_dma_fused([send(T.gu[S_FAR], T.gu, far, plane, off_b, S.lu),
                        send(T.gu[S_FAR], T.gu, far, sibs, on_a, S.mu),
                        send(T.gu[S_PL], T.gu, near, sibs, on_b, S.mu)], local_sem=S.loc)
    g.wait_ge(S.sbv, n_off)
    g.wait_ge(S.swv, n_off)
    g.remote_dma_fused([send(T.gv[S_FAR], T.gv, far, plane, off_a | off_b, S.lv),
                        send(T.gv[S_FAR], T.gv, far, sibs, on_a, S.mv),
                        send(T.gv[S_PL], T.gv, near, sibs, on_b, S.mv)], local_sem=S.lo2)
    n_lo2 = 2 * n_off + 2 * n_on

    pe = (S_MID - S_SIB) * R // 2
    pm = (S_LATE - S_MID) * R
    pl = (N_SLOT - S_LATE) * R
    for q, gbuf, ebuf, mbuf, lbuf, sa, sm, sl, nl in (
            (g.sync, T.gu, T.ue, T.um, T.ul, S.sau, S.mu, S.lu, n_off),
            (g.scalar, T.gv, T.ve, T.vm, T.vl, S.sav, S.mv, S.lv, 2 * n_off)):
        q.wait_ge(sa, n_on * len(sibs))
        q.wait_ge(S.lo2, n_lo2)
        q.dma_start(ebuf[0:pe, :], gbuf[S_SIB:S_MID]).then_inc(S.el, 16)
        q.wait_ge(sm, 2 * n_on * len(sibs))
        q.dma_start(mbuf[0:pm, :], gbuf[S_MID:S_LATE]).then_inc(S.ml, 16)
        q.wait_ge(sl, nl * len(plane))
        q.dma_start(lbuf[0:pl, :], gbuf[S_LATE:N_SLOT]).then_inc(S.ll, 16)

    w = T.pw[:, 0:D]
    g.tensor.wait_ge(S.ow, 32)
    g.tensor.matmul(w, T.uo[0:R, :], T.vo[0:R, :], start=True, stop=False)
    g.tensor.wait_ge(S.el, 32)
    for c in range(2):
        g.tensor.matmul(w, T.ue[0:pe, c * D:(c + 1) * D], T.ve[0:pe, c * D:(c + 1) * D], start=False, stop=False)
    g.tensor.wait_ge(S.ml, 32)
    g.tensor.matmul(w, T.um[0:pm, :], T.vm[0:pm, :], start=False, stop=False)
    g.tensor.wait_ge(S.ll, 32)
    g.tensor.matmul(w, T.ul[0:pl, :], T.vl[0:pl, :], start=False, stop=True).then_inc(S.mm, 1)
    g.vector.wait_ge(S.mm, 1)
    g.vector.tensor_copy(T.ws[:, :], w).then_inc(S.wc, 1)

    y = T.py[:, 0:wid]
    g.tensor.wait_ge(S.xl, 16)
    g.tensor.wait_ge(S.wc, 1)
    g.tensor.matmul(y, T.ws[:, :], T.xs[:, 0:wid], start=True, stop=True).then_inc(S.ym, 1)
    g.vector.wait_ge(S.ym, 1)
    g.vector.tensor_copy(T.ys[:, 0:wid], y).then_inc(S.yc, 1)
    g.sync.wait_ge(S.yc, 1)
    g.sync.dma_start(T.y[:, 0:wid], T.ys[:, 0:wid]).then_inc(S.st, 16)
    g.sync.wait_ge(S.st, 16)

    g.wait_ge(S.loc, 2 * (2 * n_off) + 2 * n_on + (n_off + 2 * n_on))
    g.wait_ge(S.lo2, n_lo2)
